import numpy as np
import ml_dtypes


def mxq(x, axis, fmt="e4m3"):
    dtype, down = {"e4m3": (ml_dtypes.float8_e4m3fn, 7), "e5m2": (ml_dtypes.float8_e5m2, 14)}[fmt]
    v = np.moveaxis(np.asarray(x, np.float32).astype(ml_dtypes.bfloat16).astype(np.float64), axis, -1)
    blocks = v.reshape(v.shape[:-1] + (-1, 32))
    amax = np.abs(blocks).max(-1, keepdims=True)
    byte = np.maximum(np.where(amax > 0, np.frexp(amax)[1] - 1 + 127, 0) - down, 1)
    scale = np.exp2(byte - 127.0)
    codes = (blocks / scale).astype(np.float32).astype(dtype).astype(np.float64)
    return np.moveaxis((codes * scale).reshape(v.shape), -1, axis)


WIDE = False


def mx_kscale(k):
    if not WIDE:
        return np.ones(k)
    levels = np.array([30, -30])
    if k % 512:
        return np.exp2(np.random.permutation(np.resize(levels, k // 32))).repeat(32)
    a = np.empty((k // 512, 16))
    for p in range(k // 512):
        a[p, :8] = np.random.permutation(np.resize(levels, 8))
        for g in range(8):
            far = levels[np.abs(levels - a[p, g]) >= 10]
            a[p, g + 8] = far[np.random.randint(len(far))]
    return np.exp2(a.ravel()).repeat(32)


def f64(x):
    return np.asarray(x).astype(np.float64)


def striped(idx):
    return np.tile(np.asarray(idx).reshape(-1, 16).T, (8, 1)).astype(np.uint16)


def unstriped(offs):
    return offs[:16].T.reshape(-1).astype(np.int64)


E2M1 = np.array([0.0, 0.5, 1.0, 1.5, 2.0, 3.0, 4.0, 6.0, -0.0, -0.5, -1.0, -1.5, -2.0, -3.0, -4.0, -6.0])


def pack_weight(w, fmt):
    k, n = w.shape
    w = f64(np.asarray(w, np.float32).astype(ml_dtypes.bfloat16)).reshape(k // 32, 32, n)
    amax = np.abs(w).max(1)
    if fmt in ("e4m3", "e5m2"):
        byte = np.frexp(amax)[1] - 1 + 127 - (7 if fmt == "e4m3" else 14)
    else:
        mant, ex = np.frexp(amax / 6.0)
        byte = np.where(mant > 0.5, ex, ex - 1) + 127
    byte = np.clip(np.where(amax > 0, byte, 1), 1, 254)
    scaled = (w * np.exp2(127.0 - byte)[:, None, :]).reshape(k, n).astype(np.float32)
    by_word = np.ascontiguousarray(scaled.reshape(k // 512, 128, 4, n).transpose(0, 1, 3, 2))
    if fmt in ("e4m3", "e5m2"):
        words = by_word.astype(ml_dtypes.float8_e4m3fn if fmt == "e4m3" else ml_dtypes.float8_e5m2).view(np.uint8)
    else:
        c = by_word.astype(ml_dtypes.float4_e2m1fn).view(np.uint8) & 0xF
        words = (c[..., 0::2] | (c[..., 1::2] << 4)).reshape(k // 512, 128, 2 * n)
    return np.ascontiguousarray(words), np.ascontiguousarray(byte.astype(np.uint8).reshape(k // 512, 16, n))


def unpack_weight(words, scales, fmt):
    g, _, n = scales.shape
    words = np.ascontiguousarray(words).reshape(g, 128, n, -1)
    if fmt in ("e4m3", "e5m2"):
        vals = words.view(ml_dtypes.float8_e4m3fn if fmt == "e4m3" else ml_dtypes.float8_e5m2).astype(np.float64)
    else:
        nib = np.empty((g, 128, n, 4), np.uint8)
        nib[..., 0::2] = words & 0xF
        nib[..., 1::2] = words >> 4
        vals = E2M1[nib]
    vals = vals * np.repeat(np.exp2(scales.astype(np.float64) - 127.0), 8, axis=1)[..., None]
    return vals.transpose(0, 1, 3, 2).reshape(g * 512, n)


K, T, Z, J, R, C, O, N, L, E = 512, 1024, 1024, 256, 512, 512, 256, 256, 512, 128


def setup_inputs():
    n = np.random.standard_normal
    idx = np.random.permutation(T)[:J]
    idx2 = np.random.permutation(Z)[:J]
    idx3 = np.random.permutation(C)[:J]
    idx4 = np.random.permutation(C)[:J]
    idx5 = np.random.permutation(C)[:O]
    idx6 = np.random.permutation(O)[:E]
    idx7 = np.random.permutation(O)[:E]
    fk = mx_kscale(K)
    fr = mx_kscale(R)
    fl = mx_kscale(L)
    xtp = pack_weight(n((K, T)) / fk[:, None], "e4m3")
    xop = pack_weight(n((K, Z)) / fk[:, None], "e2m1")
    wp = pack_weight(n((K, R)) * 1 / np.sqrt(K) * fk[:, None] * fr, "e5m2")
    w2p = pack_weight(n((K, R)) * 1 / np.sqrt(K) * fk[:, None] * fr, "e5m2")
    wbp = pack_weight(n((R, N)) * 1 / np.sqrt(R) / fr[:, None], "e5m2")
    sxp = pack_weight(n((L, O)) / fl[:, None], "e2m1")
    wsp = pack_weight(n((L, N)) * 1 / np.sqrt(L) * fl[:, None], "e5m2")
    return {
        "xt_words": xtp[0],
        "xt_scales": xtp[1],
        "xo_words": xop[0],
        "xo_scales": xop[1],
        "w_words": wp[0],
        "w_scales": wp[1],
        "w2_words": w2p[0],
        "w2_scales": w2p[1],
        "wb_words": wbp[0],
        "wb_scales": wbp[1],
        "sx_words": sxp[0],
        "sx_scales": sxp[1],
        "ws_words": wsp[0],
        "ws_scales": wsp[1],
        "offs": striped(idx),
        "offs2": striped(idx2),
        "offs3": striped(idx3),
        "offs4": striped(idx4),
        "offs5": striped(idx5),
        "offs6": striped(idx6),
        "offs7": striped(idx7),
    }


def reference(xt_words, xt_scales, xo_words, xo_scales, w_words, w_scales, w2_words, w2_scales, wb_words, wb_scales, sx_words, sx_scales, ws_words, ws_scales, offs, offs2, offs3, offs4, offs5, offs6, offs7):
    idx = unstriped(offs)
    idx2 = unstriped(offs2)
    idx3 = unstriped(offs3)
    idx4 = unstriped(offs4)
    idx5 = unstriped(offs5)
    idx6 = unstriped(offs6)
    idx7 = unstriped(offs7)
    xtu = unpack_weight(xt_words, xt_scales, "e4m3")
    xou = unpack_weight(xo_words, xo_scales, "e2m1")
    wu = unpack_weight(w_words, w_scales, "e5m2")
    w2u = unpack_weight(w2_words, w2_scales, "e5m2")
    wbu = unpack_weight(wb_words, wb_scales, "e5m2")
    sxu = unpack_weight(sx_words, sx_scales, "e2m1")
    wsu = unpack_weight(ws_words, ws_scales, "e5m2")
    xtidxg = xtu[:, idx]
    xoidx2g = xou[:, idx2]
    a = wu.T @ xtidxg + w2u.T @ xoidx2g
    b = w2u.T @ xtidxg + wu.T @ xoidx2g
    pw = np.zeros((R, C))
    pw[:, idx3] = a
    pv = np.zeros((R, C))
    pv[:, idx4] = b
    pg = pw + pv
    hid = pg[:, idx5]
    hidq = mxq(hid, 0, "e4m3")
    p = wbu.T @ hidq + wsu.T @ sxu
    y = np.maximum(p[:, idx6], p[:, idx7])
    return y

@@ -1,0 +1,220 @@
+from contextlib import ExitStack
+
+import concourse.mybir as mybir
+
+K, T, Z, J, R, C, O, N, L, E = 512, 1024, 1024, 256, 512, 512, 256, 256, 512, 128
+FLOPS = 2 * (2 * 2 * K * R * J + R * N * O + L * N * O)
+
+F32 = mybir.dt.float32
+BF16 = mybir.dt.bfloat16
+I32 = mybir.dt.int32
+U32 = mybir.dt.uint32
+U16 = mybir.dt.uint16
+U8 = mybir.dt.uint8
+E4M3 = mybir.dt.float8_e4m3fn_x4
+E5M2 = mybir.dt.float8_e5m2_x4
+E2M1 = mybir.dt.float4_e2m1fn_x4
+COPY = mybir.ActivationFunctionType.Copy
+ADD = mybir.AluOpType.add
+MAX = mybir.AluOpType.max
+
+P = 128
+PACK = 4
+QUAD = 32
+GROUP = 16
+HANDED = 64
+
+
+def tile_list_crossed_shared_skip_bestoftwo_kernel(
+    tc, xt_words, xt_scales, xo_words, xo_scales, w_words, w_scales, w2_words, w2_scales,
+    wb_words, wb_scales, sx_words, sx_scales, ws_words, ws_scales,
+    offs, offs2, offs3, offs4, offs5, offs6, offs7, out,
+):
+    nc = tc.nc
+    with ExitStack() as ctx:
+        sb = ctx.enter_context(tc.tile_pool(name="sb", bufs=1))
+        ps = ctx.enter_context(tc.psum_pool(name="ps", bufs=1))
+
+        def tile(name, shape, dtype, tag=""):
+            return sb.tile(shape, dtype, name=name, tag=tag or name, align_bytes=64)
+
+        def load_list(name, src):
+            t = sb.tile(list(src.shape), U16, name=name)
+            nc.sync.dma_start(t[:], src)
+            return t
+
+        def load_words(queue, dst, src):
+            flat = src[0] if src.ndim == 3 else src[0].rearrange("p c t -> p (c t)")
+            queue.dma_start(dst.bitcast(I32), flat.bitcast(I32))
+
+        def load_scales(queue, dst, src, rows):
+            for r in rows:
+                queue.dma_start(dst[r:P:QUAD, :].bitcast(I32), src[0, r::PACK, :].bitcast(I32))
+
+        xt_w, xt_s = tile("xt_w", [P, T], U32), tile("xt_s", [P, T], U8)
+        xo_w, xo_s = tile("xo_w", [P, Z], U16), tile("xo_s", [P, Z], U8)
+        w_raw, w2_raw = tile("w_raw", [P, R], U32), tile("w2_raw", [P, R], U32)
+        raw_s = tile("raw_s", [P, 2 * R], U8)
+        w_sraw, w2_sraw = raw_s[:, 0:R], raw_s[:, R:]
+        ws_w, ws_s = tile("ws_w", [P, N], U32), tile("ws_s", [P, N], U8)
+        wb_w, wb_s = tile("wb_w", [P, N], U32), tile("wb_s", [P, N], U8)
+        sx_w, sx_s = tile("sx_w", [P, O], U16), tile("sx_s", [P, O], U8)
+        nc.vector.memset(xt_s[:].bitcast(I32), 0)
+        nc.gpsimd.memset(xo_s[:].bitcast(I32), 0)
+        nc.gpsimd.memset(raw_s[:].bitcast(I32), 0)
+        l1 = load_list("l1", offs)
+        l2 = load_list("l2", offs2)
+        load_scales(nc.sync, xt_s[:], xt_scales, range(PACK))
+        load_words(nc.sync, xo_w[:], xo_words)
+        load_words(nc.sync, xt_w[:], xt_words)
+        load_scales(nc.sync, xo_s[:], xo_scales, range(PACK))
+        load_scales(nc.sync, w_sraw, w_scales, range(0, 2))
+        load_words(nc.sync, w_raw[:], w_words)
+        load_words(nc.sync, w2_raw[:], w2_words)
+        load_scales(nc.sync, w_sraw, w_scales, range(2, 4))
+        load_scales(nc.sync, w2_sraw, w2_scales, range(PACK))
+        l3 = load_list("l3", offs3)
+        l4 = load_list("l4", offs4)
+        l5 = load_list("l5", offs5)
+        load_words(nc.sync, ws_w[:], ws_words)
+        load_words(nc.sync, sx_w[:], sx_words)
+        load_words(nc.sync, wb_w[:], wb_words)
+        load_scales(nc.sync, ws_s[:], ws_scales, range(PACK))
+        load_scales(nc.sync, sx_s[:], sx_scales, range(PACK))
+        load_scales(nc.sync, wb_s[:], wb_scales, range(PACK))
+        l6 = load_list("l6", offs6)
+        l7 = load_list("l7", offs7)
+
+        pw = [tile(f"pw{t}", [P, C], F32) for t in range(PACK)]
+        pv = [tile(f"pv{t}", [P, C], F32) for t in range(PACK)]
+        for t in range(PACK):
+            nc.vector.memset(pw[t][:], 0.0)
+            nc.vector.memset(pv[t][:], 0.0)
+
+        xtg_w = tile("xtg_w", [P, J], U32)
+        xtg_s = tile("xtg_s", [P, J], U8)
+        xog_w = tile("xog_w", [P, J], U16)
+        xog_s = tile("xog_s", [P, J], U8)
+        nc.vector.tensor_copy(xtg_s[:], xt_s[:].indirect(l1[:]))
+        nc.vector.tensor_copy(xog_w[:], xo_w[:].indirect(l2[:]))
+        nc.vector.tensor_copy(xtg_w[:], xt_w[:].indirect(l1[:]))
+        nc.vector.tensor_copy(xog_s[:], xo_s[:].indirect(l2[:]))
+        xt_op = (xtg_w[:].bitcast(E4M3), xtg_s[:])
+        xo_op = (xog_w[:].bitcast(E2M1), xog_s[:])
+
+        def dealt(engine, name, raw, dtype, first, last):
+            parts = raw.shape[1] // R
+            d = tile(name, [P, parts, last - first, P], dtype)
+            engine.tensor_copy(d[:], raw.rearrange("p (u m t) -> p u t m", u=parts, t=PACK)[:, :, first:last, :])
+            return [[d[:, u, i, :] for u in range(parts)] for i in range(last - first)]
+
+        w_w = dealt(nc.vector, "w_w", w_raw[:], U32, 0, PACK)
+        w2_w = dealt(nc.vector, "w2_w0", w2_raw[:], U32, 0, 1)
+        sc = dealt(nc.vector, "sc0", raw_s[:], U8, 0, 1)
+        w2_w = w2_w + dealt(nc.gpsimd, "w2_w1", w2_raw[:], U32, 1, PACK)
+        for t in range(1, PACK):
+            sc = sc + dealt(nc.gpsimd, f"sc{t}", raw_s[:], U8, t, t + 1)
+        w_op = [(w_w[t][0].bitcast(E5M2), sc[t][0]) for t in range(PACK)]
+        w2_op = [(w2_w[t][0].bitcast(E5M2), sc[t][1]) for t in range(PACK)]
+
+        def mm(dst, stat, mov, start, stop):
+            nc.tensor.matmul_mx(out=dst, lhsT=stat[0], lhsT_scale=stat[1], rhs=mov[0], rhs_scale=mov[1], start=start, stop=stop)
+
+        def sum_a(dst, t):
+            mm(dst, w_op[t], xt_op, True, False)
+            mm(dst, w2_op[t], xo_op, False, True)
+
+        def sum_b(dst, t):
+            mm(dst, w2_op[t], xt_op, True, False)
+            mm(dst, w_op[t], xo_op, False, True)
+
+        a_sb, b_sb = [None] * PACK, [None] * PACK
+
+        def alone(kind, t, engine_copy):
+            bank = ps.tile([P, J], F32, name=f"{kind}{t}")
+            (sum_a if kind == "a" else sum_b)(bank[:], t)
+            staged = tile(f"{kind}_sb{t}", [P, J], F32)
+            engine_copy(staged[:], bank[:])
+            (a_sb if kind == "a" else b_sb)[t] = staged[:]
+
+        def paired(t):
+            bank = ps.tile([P, 2 * J], F32, name=f"ab{t}")
+            sum_a(bank[:, 0:J], t)
+            sum_b(bank[:, J:], t)
+            staged = tile(f"ab_sb{t}", [P, 2 * J], F32)
+            nc.scalar.copy(staged[:], bank[:])
+            a_sb[t], b_sb[t] = staged[:, 0:J], staged[:, J:]
+
+        def put_a(t):
+            nc.scalar.activation(out=pw[t][:].indirect(l3[:]), in_=a_sb[t], func=COPY)
+
+        def put_b(t):
+            if t < PACK - 1 or HANDED == 0:
+                nc.vector.tensor_copy(pv[t][:].indirect(l4[:]), b_sb[t])
+            else:
+                cut = J - HANDED
+                nc.vector.tensor_copy(pv[t][:].indirect(l4[:, 0 : cut // GROUP]), b_sb[t][:, 0:cut])
+                nc.scalar.activation(out=pv[t][:].indirect(l4[:, cut // GROUP :]), in_=b_sb[t][:, cut:], func=COPY)
+
+        hid = tile("hid", [P, O * PACK], BF16)
+        halves = 2
+        half = O // halves
+
+        def read_board(t):
+            pg = tile(f"pg{t}", [P, C], F32, tag=f"pg{min(t, PACK - 2)}")
+            eng = nc.vector if t == PACK - 1 else nc.gpsimd
+            eng.tensor_tensor(pg[:], pw[t][:], pv[t][:], ADD)
+            if t < PACK - 1:
+                nc.vector.tensor_copy(hid[:, t::PACK], pg[:].indirect(l5[:]))
+            else:
+                for u in range(halves):
+                    dst = hid[:, PACK * half * u + t : PACK * half * (u + 1) : PACK]
+                    nc.vector.tensor_copy(dst, pg[:].indirect(l5[:, half // GROUP * u : half // GROUP * (u + 1)]))
+
+        alone("a", 0, nc.scalar.copy)
+        alone("b", 0, nc.vector.tensor_copy)
+        put_a(0)
+        put_b(0)
+        alone("b", 1, nc.vector.tensor_copy)
+        alone("a", 1, nc.scalar.copy)
+        paired(2)
+        put_b(1)
+        put_a(1)
+        paired(3)
+        put_b(2)
+        put_a(2)
+        put_a(3)
+        put_b(3)
+
+        p_ps = [ps.tile([P, O], F32, name=f"p{h}") for h in range(N // P)]
+        for h in range(N // P):
+            cols = slice(P * h, P * (h + 1))
+            mm(p_ps[h][:], (ws_w[:, cols].bitcast(E5M2), ws_s[:, cols]), (sx_w[:].bitcast(E2M1), sx_s[:]), True, False)
+
+        for t in range(PACK):
+            read_board(t)
+
+        for u in range(halves):
+            hid_w = tile(f"hid_w{u}", [P, half], U32)
+            hid_s = tile(f"hid_s{u}", [P, half], U8)
+            nc.vector.quantize_mx(out=hid_w[:].bitcast(E4M3), scales=hid_s[:], in_=hid[:, PACK * half * u : PACK * half * (u + 1)])
+            for h in range(N // P):
+                cols = slice(P * h, P * (h + 1))
+                mm(p_ps[h][:, half * u : half * (u + 1)], (wb_w[:, cols].bitcast(E5M2), wb_s[:, cols]),
+                   (hid_w[:].bitcast(E4M3), hid_s[:]), False, u == halves - 1)
+
+        for h in range(N // P):
+            p_sb = tile(f"p_sb{h}", [P, O], F32)
+            g6 = tile(f"g6_{h}", [P, E], F32)
+            g7 = tile(f"g7_{h}", [P, E], F32)
+            res = tile(f"res{h}", [P, E], F32)
+            if h == 0:
+                nc.scalar.copy(p_sb[:], p_ps[h][:])
+                nc.scalar.activation(out=g6[:], in_=p_sb[:].indirect(l6[:]), func=COPY)
+                nc.scalar.activation(out=g7[:], in_=p_sb[:].indirect(l7[:]), func=COPY)
+            else:
+                nc.vector.tensor_copy(p_sb[:], p_ps[h][:])
+                nc.vector.tensor_copy(g6[:], p_sb[:].indirect(l6[:]))
+                nc.vector.tensor_copy(g7[:], p_sb[:].indirect(l7[:]))
+            nc.vector.tensor_tensor(res[:], g6[:], g7[:], MAX)
+            nc.sync.dma_start(out[P * h : P * (h + 1), :], res[:])

@@ -22,7 +22,7 @@ P = 128
 PACK = 4
 QUAD = 32
 GROUP = 16
-HANDED = 64
+HANDED = 0
 
 
 def tile_list_crossed_shared_skip_bestoftwo_kernel(
@@ -110,7 +110,7 @@ def tile_list_crossed_shared_skip_bestoftwo_kernel(
 
         w_w = dealt(nc.vector, "w_w", w_raw[:], U32, 0, PACK)
         w2_w = dealt(nc.vector, "w2_w0", w2_raw[:], U32, 0, 1)
-        sc = dealt(nc.vector, "sc0", raw_s[:], U8, 0, 1)
+        sc = [dealt(nc.vector, "w_s0", w_sraw, U8, 0, 1)[0] + dealt(nc.vector, "w2_s0", w2_sraw, U8, 0, 1)[0]]
         w2_w = w2_w + dealt(nc.gpsimd, "w2_w1", w2_raw[:], U32, 1, PACK)
         for t in range(1, PACK):
             sc = sc + dealt(nc.gpsimd, f"sc{t}", raw_s[:], U8, t, t + 1)
@@ -128,22 +128,16 @@ def tile_list_crossed_shared_skip_bestoftwo_kernel(
             mm(dst, w2_op[t], xt_op, True, False)
             mm(dst, w_op[t], xo_op, False, True)
 
-        a_sb, b_sb = [None] * PACK, [None] * PACK
-
-        def alone(kind, t, engine_copy):
-            bank = ps.tile([P, J], F32, name=f"{kind}{t}")
-            (sum_a if kind == "a" else sum_b)(bank[:], t)
-            staged = tile(f"{kind}_sb{t}", [P, J], F32)
-            engine_copy(staged[:], bank[:])
-            (a_sb if kind == "a" else b_sb)[t] = staged[:]
-
-        def paired(t):
-            bank = ps.tile([P, 2 * J], F32, name=f"ab{t}")
-            sum_a(bank[:, 0:J], t)
-            sum_b(bank[:, J:], t)
-            staged = tile(f"ab_sb{t}", [P, 2 * J], F32)
-            nc.scalar.copy(staged[:], bank[:])
-            a_sb[t], b_sb[t] = staged[:, 0:J], staged[:, J:]
+        a_ps, b_ps = ps.tile([P, J], F32, name="a0", tag="a0"), ps.tile([P, J], F32, name="b0", tag="b0")
+        mm(a_ps[:], w_op[0], xt_op, True, False)
+        mm(b_ps[:], w_op[0], xo_op, True, False)
+        mm(a_ps[:], w2_op[0], xo_op, False, True)
+        mm(b_ps[:], w2_op[0], xt_op, False, True)
+        first_a = tile("first_a", [P, J], F32, tag="staged")
+        first_b = tile("first_b", [P, J], F32)
+        nc.scalar.copy(first_a[:], a_ps[:])
+        nc.vector.tensor_copy(first_b[:], b_ps[:])
+        a_sb, b_sb = [first_a[:]], [first_b[:]]
 
         def put_a(t):
             nc.scalar.activation(out=pw[t][:].indirect(l3[:]), in_=a_sb[t], func=COPY)
@@ -156,52 +150,74 @@ def tile_list_crossed_shared_skip_bestoftwo_kernel(
                 nc.vector.tensor_copy(pv[t][:].indirect(l4[:, 0 : cut // GROUP]), b_sb[t][:, 0:cut])
                 nc.scalar.activation(out=pv[t][:].indirect(l4[:, cut // GROUP :]), in_=b_sb[t][:, cut:], func=COPY)
 
-        hid = tile("hid", [P, O * PACK], BF16)
         halves = 2
         half = O // halves
+        planes = tile("planes", [P, PACK * O], BF16)
+        boards = []
 
-        def read_board(t):
-            pg = tile(f"pg{t}", [P, C], F32, tag=f"pg{min(t, PACK - 2)}")
+        def join(t):
+            pg = tile(f"pg{t}", [P, C], F32, tag=f"pg{t % (PACK - 2) if t == PACK - 1 else t}")
             eng = nc.vector if t == PACK - 1 else nc.gpsimd
             eng.tensor_tensor(pg[:], pw[t][:], pv[t][:], ADD)
-            if t < PACK - 1:
-                nc.vector.tensor_copy(hid[:, t::PACK], pg[:].indirect(l5[:]))
-            else:
-                for u in range(halves):
-                    dst = hid[:, PACK * half * u + t : PACK * half * (u + 1) : PACK]
-                    nc.vector.tensor_copy(dst, pg[:].indirect(l5[:, half // GROUP * u : half // GROUP * (u + 1)]))
+            boards.append(pg)
 
-        alone("a", 0, nc.scalar.copy)
-        alone("b", 0, nc.vector.tensor_copy)
+        def read_board(t):
+            pg = boards[t]
+            if t == PACK - 2:
+                nc.scalar.activation(out=planes[:, O * t : O * (t + 1)], in_=pg[:].indirect(l5[:]), func=COPY)
+            elif t < PACK - 1:
+                nc.vector.tensor_copy(planes[:, O * t : O * (t + 1)], pg[:].indirect(l5[:]))
+            else:
+                nc.vector.tensor_copy(planes[:, O * t : O * t + half], pg[:].indirect(l5[:, 0 : half // GROUP]))
+                nc.scalar.activation(out=planes[:, O * t + half :], in_=pg[:].indirect(l5[:, half // GROUP :]), func=COPY)
+
         put_a(0)
         put_b(0)
-        alone("b", 1, nc.vector.tensor_copy)
-        alone("a", 1, nc.scalar.copy)
-        paired(2)
-        put_b(1)
-        put_a(1)
-        paired(3)
-        put_b(2)
-        put_a(2)
-        put_a(3)
-        put_b(3)
+        later = tile("later", [P, (PACK - 1) * 2 * J], F32, tag="staged")
+        for t in range(1, PACK):
+            a_sb.append(later[:, (2 * t - 2) * J : (2 * t - 1) * J])
+            b_sb.append(later[:, (2 * t - 1) * J : 2 * t * J])
+        a_ps, b_ps = ps.tile([P, J], F32, name="a1"), ps.tile([P, J], F32, name="b1")
+        sum_b(b_ps[:], 1)
+        sum_a(a_ps[:], 1)
+        nc.scalar.copy(b_sb[1], b_ps[:])
+        nc.scalar.copy(a_sb[1], a_ps[:])
+        for t in range(2, PACK):
+            bank = ps.tile([P, 2 * J], F32, name=f"ab{t}")
+            sum_a(bank[:, 0:J], t)
+            sum_b(bank[:, J:], t)
+            nc.scalar.copy(later[:, (2 * t - 2) * J : 2 * t * J], bank[:])
+        for t in range(1, PACK):
+            put_a(t)
+            put_b(t)
 
-        p_ps = [ps.tile([P, O], F32, name=f"p{h}") for h in range(N // P)]
-        for h in range(N // P):
-            cols = slice(P * h, P * (h + 1))
-            mm(p_ps[h][:], (ws_w[:, cols].bitcast(E5M2), ws_s[:, cols]), (sx_w[:].bitcast(E2M1), sx_s[:]), True, False)
+        p_ps = [[ps.tile([P, half], F32, name=f"p{h}{u}", tag=("a0", "b0")[h] if u == 0 else f"p{h}") for u in range(halves)] for h in range(N // P)]
+        for u in range(halves):
+            reads = slice(half * u, half * (u + 1))
+            for h in range(N // P):
+                cols = slice(P * h, P * (h + 1))
+                mm(p_ps[h][u][:], (ws_w[:, cols].bitcast(E5M2), ws_s[:, cols]), (sx_w[:, reads].bitcast(E2M1), sx_s[:, reads]), True, False)
 
         for t in range(PACK):
+            join(t)
             read_board(t)
 
+        woven = []
+        for u in range(halves):
+            hid = tile(f"hid{u}", [P, half * PACK], BF16)
+            src = planes[:].rearrange("p (t o) -> p t o", t=PACK)[:, :, half * u : half * (u + 1)]
+            nc.vector.tensor_copy(
+                hid[:].rearrange("p (c i t) -> p c t i", i=PACK, t=PACK), src.rearrange("p t (c i) -> p c t i", i=PACK)
+            )
+            woven.append(hid)
         for u in range(halves):
             hid_w = tile(f"hid_w{u}", [P, half], U32)
             hid_s = tile(f"hid_s{u}", [P, half], U8)
-            nc.vector.quantize_mx(out=hid_w[:].bitcast(E4M3), scales=hid_s[:], in_=hid[:, PACK * half * u : PACK * half * (u + 1)])
+            nc.vector.quantize_mx(out=hid_w[:].bitcast(E4M3), scales=hid_s[:], in_=woven[u][:])
             for h in range(N // P):
                 cols = slice(P * h, P * (h + 1))
-                mm(p_ps[h][:, half * u : half * (u + 1)], (wb_w[:, cols].bitcast(E5M2), wb_s[:, cols]),
-                   (hid_w[:].bitcast(E4M3), hid_s[:]), False, u == halves - 1)
+                mm(p_ps[h][u][:], (wb_w[:, cols].bitcast(E5M2), wb_s[:, cols]),
+                   (hid_w[:].bitcast(E4M3), hid_s[:]), False, True)
 
         for h in range(N // P):
             p_sb = tile(f"p_sb{h}", [P, O], F32)
@@ -209,11 +225,13 @@ def tile_list_crossed_shared_skip_bestoftwo_kernel(
             g7 = tile(f"g7_{h}", [P, E], F32)
             res = tile(f"res{h}", [P, E], F32)
             if h == 0:
-                nc.scalar.copy(p_sb[:], p_ps[h][:])
+                for u in range(halves):
+                    nc.scalar.copy(p_sb[:, half * u : half * (u + 1)], p_ps[h][u][:])
                 nc.scalar.activation(out=g6[:], in_=p_sb[:].indirect(l6[:]), func=COPY)
                 nc.scalar.activation(out=g7[:], in_=p_sb[:].indirect(l7[:]), func=COPY)
             else:
-                nc.vector.tensor_copy(p_sb[:], p_ps[h][:])
+                for u in range(halves):
+                    nc.vector.tensor_copy(p_sb[:, half * u : half * (u + 1)], p_ps[h][u][:])
                 nc.vector.tensor_copy(g6[:], p_sb[:].indirect(l6[:]))
                 nc.vector.tensor_copy(g7[:], p_sb[:].indirect(l7[:]))
             nc.vector.tensor_tensor(res[:], g6[:], g7[:], MAX)

@@ -22,7 +22,6 @@ P = 128
 PACK = 4
 QUAD = 32
 GROUP = 16
-HANDED = 0
 
 
 def tile_list_crossed_shared_skip_bestoftwo_kernel(
@@ -59,14 +58,13 @@ def tile_list_crossed_shared_skip_bestoftwo_kernel(
         ws_w, ws_s = tile("ws_w", [P, N], U32), tile("ws_s", [P, N], U8)
         wb_w, wb_s = tile("wb_w", [P, N], U32), tile("wb_s", [P, N], U8)
         sx_w, sx_s = tile("sx_w", [P, O], U16), tile("sx_s", [P, O], U8)
-        nc.vector.memset(xt_s[:].bitcast(I32), 0)
-        nc.gpsimd.memset(xo_s[:].bitcast(I32), 0)
-        nc.gpsimd.memset(raw_s[:].bitcast(I32), 0)
+        for plane in (xt_s, xo_s, raw_s):
+            nc.vector.memset(plane[:].bitcast(I32), 0)
         l1 = load_list("l1", offs)
         l2 = load_list("l2", offs2)
         load_scales(nc.sync, xt_s[:], xt_scales, range(PACK))
-        load_words(nc.sync, xo_w[:], xo_words)
         load_words(nc.sync, xt_w[:], xt_words)
+        load_words(nc.sync, xo_w[:], xo_words)
         load_scales(nc.sync, xo_s[:], xo_scales, range(PACK))
         load_scales(nc.sync, w_sraw, w_scales, range(0, 2))
         load_words(nc.sync, w_raw[:], w_words)
@@ -96,8 +94,8 @@ def tile_list_crossed_shared_skip_bestoftwo_kernel(
         xog_w = tile("xog_w", [P, J], U16)
         xog_s = tile("xog_s", [P, J], U8)
         nc.vector.tensor_copy(xtg_s[:], xt_s[:].indirect(l1[:]))
-        nc.vector.tensor_copy(xog_w[:], xo_w[:].indirect(l2[:]))
         nc.vector.tensor_copy(xtg_w[:], xt_w[:].indirect(l1[:]))
+        nc.vector.tensor_copy(xog_w[:], xo_w[:].indirect(l2[:]))
         nc.vector.tensor_copy(xog_s[:], xo_s[:].indirect(l2[:]))
         xt_op = (xtg_w[:].bitcast(E4M3), xtg_s[:])
         xo_op = (xog_w[:].bitcast(E2M1), xog_s[:])
@@ -133,8 +131,8 @@ def tile_list_crossed_shared_skip_bestoftwo_kernel(
         mm(b_ps[:], w_op[0], xo_op, True, False)
         mm(a_ps[:], w2_op[0], xo_op, False, True)
         mm(b_ps[:], w2_op[0], xt_op, False, True)
-        first_a = tile("first_a", [P, J], F32, tag="staged")
-        first_b = tile("first_b", [P, J], F32)
+        first_a = tile("first_a", [P, J], F32, tag="staged_a")
+        first_b = tile("first_b", [P, J], F32, tag="staged_b")
         nc.scalar.copy(first_a[:], a_ps[:])
         nc.vector.tensor_copy(first_b[:], b_ps[:])
         a_sb, b_sb = [first_a[:]], [first_b[:]]
@@ -143,50 +141,26 @@ def tile_list_crossed_shared_skip_bestoftwo_kernel(
             nc.scalar.activation(out=pw[t][:].indirect(l3[:]), in_=a_sb[t], func=COPY)
 
         def put_b(t):
-            if t < PACK - 1 or HANDED == 0:
-                nc.vector.tensor_copy(pv[t][:].indirect(l4[:]), b_sb[t])
-            else:
-                cut = J - HANDED
-                nc.vector.tensor_copy(pv[t][:].indirect(l4[:, 0 : cut // GROUP]), b_sb[t][:, 0:cut])
-                nc.scalar.activation(out=pv[t][:].indirect(l4[:, cut // GROUP :]), in_=b_sb[t][:, cut:], func=COPY)
+            nc.vector.tensor_copy(pv[t][:].indirect(l4[:]), b_sb[t])
 
         halves = 2
         half = O // halves
-        planes = tile("planes", [P, PACK * O], BF16)
-        boards = []
-
-        def join(t):
-            pg = tile(f"pg{t}", [P, C], F32, tag=f"pg{t % (PACK - 2) if t == PACK - 1 else t}")
-            eng = nc.vector if t == PACK - 1 else nc.gpsimd
-            eng.tensor_tensor(pg[:], pw[t][:], pv[t][:], ADD)
-            boards.append(pg)
-
-        def read_board(t):
-            pg = boards[t]
-            if t == PACK - 2:
-                nc.scalar.activation(out=planes[:, O * t : O * (t + 1)], in_=pg[:].indirect(l5[:]), func=COPY)
-            elif t < PACK - 1:
-                nc.vector.tensor_copy(planes[:, O * t : O * (t + 1)], pg[:].indirect(l5[:]))
-            else:
-                nc.vector.tensor_copy(planes[:, O * t : O * t + half], pg[:].indirect(l5[:, 0 : half // GROUP]))
-                nc.scalar.activation(out=planes[:, O * t + half :], in_=pg[:].indirect(l5[:, half // GROUP :]), func=COPY)
+        last = PACK - 1
 
         put_a(0)
         put_b(0)
-        later = tile("later", [P, (PACK - 1) * 2 * J], F32, tag="staged")
-        for t in range(1, PACK):
-            a_sb.append(later[:, (2 * t - 2) * J : (2 * t - 1) * J])
-            b_sb.append(later[:, (2 * t - 1) * J : 2 * t * J])
-        a_ps, b_ps = ps.tile([P, J], F32, name="a1"), ps.tile([P, J], F32, name="b1")
-        sum_b(b_ps[:], 1)
-        sum_a(a_ps[:], 1)
-        nc.scalar.copy(b_sb[1], b_ps[:])
-        nc.scalar.copy(a_sb[1], a_ps[:])
-        for t in range(2, PACK):
-            bank = ps.tile([P, 2 * J], F32, name=f"ab{t}")
-            sum_a(bank[:, 0:J], t)
-            sum_b(bank[:, J:], t)
-            nc.scalar.copy(later[:, (2 * t - 2) * J : 2 * t * J], bank[:])
+
+        def later_sums(kind, summed, copy, staged):
+            later = tile(f"later_{kind}", [P, last * J], F32, tag=f"staged_{kind}")
+            for first, stop in ((1, last), (last, PACK)):
+                bank = ps.tile([P, (stop - first) * J], F32, name=f"{kind}{first}")
+                for t in range(first, stop):
+                    summed(bank[:, (t - first) * J : (t - first + 1) * J], t)
+                    staged.append(later[:, (t - 1) * J : t * J])
+                copy(later[:, (first - 1) * J : (stop - 1) * J], bank[:])
+
+        later_sums("a", sum_a, nc.scalar.copy, a_sb)
+        later_sums("b", sum_b, nc.vector.tensor_copy, b_sb)
         for t in range(1, PACK):
             put_a(t)
             put_b(t)
@@ -198,18 +172,20 @@ def tile_list_crossed_shared_skip_bestoftwo_kernel(
                 cols = slice(P * h, P * (h + 1))
                 mm(p_ps[h][u][:], (ws_w[:, cols].bitcast(E5M2), ws_s[:, cols]), (sx_w[:, reads].bitcast(E2M1), sx_s[:, reads]), True, False)
 
+        pg = [tile(f"pg{t}", [P, C], F32) for t in range(PACK)]
         for t in range(PACK):
-            join(t)
-            read_board(t)
+            (nc.vector if t == last else nc.gpsimd).tensor_tensor(pg[t][:], pw[t][:], pv[t][:], ADD)
+        low = tile("low", [P, 2 * O], BF16, tag="staged_a")
+        high = tile("high", [P, 2 * O], BF16, tag="staged_b")
+        for t, dst in enumerate((low[:, 0:O], low[:, O:], high[:, 0:O])):
+            nc.scalar.activation(out=dst, in_=pg[t][:].indirect(l5[:]), func=COPY)
+        nc.vector.tensor_copy(high[:, O:], pg[last][:].indirect(l5[:]))
 
-        woven = []
-        for u in range(halves):
-            hid = tile(f"hid{u}", [P, half * PACK], BF16)
-            src = planes[:].rearrange("p (t o) -> p t o", t=PACK)[:, :, half * u : half * (u + 1)]
-            nc.vector.tensor_copy(
-                hid[:].rearrange("p (c i t) -> p c t i", i=PACK, t=PACK), src.rearrange("p t (c i) -> p c t i", i=PACK)
-            )
-            woven.append(hid)
+        woven = [tile(f"hid{u}", [P, half * PACK], BF16, tag=(f"pv{last}", f"pw{last}")[u]) for u in range(halves)]
+        for i, pair in enumerate((low, high)):
+            for u in range(halves):
+                src = pair[:].rearrange("p (e o) -> p o e", e=2)[:, half * u : half * (u + 1), :]
+                nc.vector.tensor_copy(woven[u][:].rearrange("p (o t) -> p o t", t=PACK)[:, :, 2 * i : 2 * i + 2], src)
         for u in range(halves):
             hid_w = tile(f"hid_w{u}", [P, half], U32)
             hid_s = tile(f"hid_s{u}", [P, half], U8)

from contextlib import ExitStack

import concourse.mybir as mybir

K, T, Z, J, R, C, O, N, L, E = 512, 1024, 1024, 256, 512, 512, 256, 256, 512, 128
FLOPS = 2 * (2 * 2 * K * R * J + R * N * O + L * N * O)

F32 = mybir.dt.float32
BF16 = mybir.dt.bfloat16
I32 = mybir.dt.int32
U32 = mybir.dt.uint32
U16 = mybir.dt.uint16
U8 = mybir.dt.uint8
E4M3 = mybir.dt.float8_e4m3fn_x4
E5M2 = mybir.dt.float8_e5m2_x4
E2M1 = mybir.dt.float4_e2m1fn_x4
COPY = mybir.ActivationFunctionType.Copy
ADD = mybir.AluOpType.add
MAX = mybir.AluOpType.max

P = 128
PACK = 4
QUAD = 32
GROUP = 16


def tile_list_crossed_shared_skip_bestoftwo_kernel(
    tc, xt_words, xt_scales, xo_words, xo_scales, w_words, w_scales, w2_words, w2_scales,
    wb_words, wb_scales, sx_words, sx_scales, ws_words, ws_scales,
    offs, offs2, offs3, offs4, offs5, offs6, offs7, out,
):
    nc = tc.nc
    with ExitStack() as ctx:
        sb = ctx.enter_context(tc.tile_pool(name="sb", bufs=1))
        ps = ctx.enter_context(tc.psum_pool(name="ps", bufs=1))

        def tile(name, shape, dtype, tag=""):
            return sb.tile(shape, dtype, name=name, tag=tag or name, align_bytes=64)

        def load_list(name, src):
            t = sb.tile(list(src.shape), U16, name=name)
            nc.sync.dma_start(t[:], src)
            return t

        def load_words(queue, dst, src):
            flat = src[0] if src.ndim == 3 else src[0].rearrange("p c t -> p (c t)")
            queue.dma_start(dst.bitcast(I32), flat.bitcast(I32))

        def load_scales(queue, dst, src, rows):
            for r in rows:
                queue.dma_start(dst[r:P:QUAD, :].bitcast(I32), src[0, r::PACK, :].bitcast(I32))

        xt_w, xt_s = tile("xt_w", [P, T], U32), tile("xt_s", [P, T], U8)
        xo_w, xo_s = tile("xo_w", [P, Z], U16), tile("xo_s", [P, Z], U8)
        w_raw, w2_raw = tile("w_raw", [P, R], U32), tile("w2_raw", [P, R], U32)
        raw_s = tile("raw_s", [P, 2 * R], U8)
        w_sraw, w2_sraw = raw_s[:, 0:R], raw_s[:, R:]
        ws_w, ws_s = tile("ws_w", [P, N], U32), tile("ws_s", [P, N], U8)
        wb_w, wb_s = tile("wb_w", [P, N], U32), tile("wb_s", [P, N], U8)
        sx_w, sx_s = tile("sx_w", [P, O], U16), tile("sx_s", [P, O], U8)
        for plane in (xt_s, xo_s, raw_s):
            nc.vector.memset(plane[:].bitcast(I32), 0)
        l1 = load_list("l1", offs)
        l2 = load_list("l2", offs2)
        load_scales(nc.sync, xt_s[:], xt_scales, range(PACK))
        load_words(nc.sync, xt_w[:], xt_words)
        load_words(nc.sync, xo_w[:], xo_words)
        load_scales(nc.sync, xo_s[:], xo_scales, range(PACK))
        load_scales(nc.sync, w_sraw, w_scales, range(0, 2))
        load_words(nc.sync, w_raw[:], w_words)
        load_words(nc.sync, w2_raw[:], w2_words)
        load_scales(nc.sync, w_sraw, w_scales, range(2, 4))
        load_scales(nc.sync, w2_sraw, w2_scales, range(PACK))
        l3 = load_list("l3", offs3)
        l4 = load_list("l4", offs4)
        l5 = load_list("l5", offs5)
        load_words(nc.sync, ws_w[:], ws_words)
        load_words(nc.sync, sx_w[:], sx_words)
        load_words(nc.sync, wb_w[:], wb_words)
        load_scales(nc.sync, ws_s[:], ws_scales, range(PACK))
        load_scales(nc.sync, sx_s[:], sx_scales, range(PACK))
        load_scales(nc.sync, wb_s[:], wb_scales, range(PACK))
        l6 = load_list("l6", offs6)
        l7 = load_list("l7", offs7)

        pw = [tile(f"pw{t}", [P, C], F32) for t in range(PACK)]
        pv = [tile(f"pv{t}", [P, C], F32) for t in range(PACK)]
        for t in range(PACK):
            nc.vector.memset(pw[t][:], 0.0)
            nc.vector.memset(pv[t][:], 0.0)

        xtg_w = tile("xtg_w", [P, J], U32)
        xtg_s = tile("xtg_s", [P, J], U8)
        xog_w = tile("xog_w", [P, J], U16)
        xog_s = tile("xog_s", [P, J], U8)
        nc.vector.tensor_copy(xtg_s[:], xt_s[:].indirect(l1[:]))
        nc.vector.tensor_copy(xtg_w[:], xt_w[:].indirect(l1[:]))
        nc.vector.tensor_copy(xog_w[:], xo_w[:].indirect(l2[:]))
        nc.vector.tensor_copy(xog_s[:], xo_s[:].indirect(l2[:]))
        xt_op = (xtg_w[:].bitcast(E4M3), xtg_s[:])
        xo_op = (xog_w[:].bitcast(E2M1), xog_s[:])

        def dealt(engine, name, raw, dtype, first, last):
            parts = raw.shape[1] // R
            d = tile(name, [P, parts, last - first, P], dtype)
            engine.tensor_copy(d[:], raw.rearrange("p (u m t) -> p u t m", u=parts, t=PACK)[:, :, first:last, :])
            return [[d[:, u, i, :] for u in range(parts)] for i in range(last - first)]

        w_w = dealt(nc.vector, "w_w", w_raw[:], U32, 0, PACK)
        w2_w = dealt(nc.vector, "w2_w0", w2_raw[:], U32, 0, 1)
        sc = [dealt(nc.vector, "w_s0", w_sraw, U8, 0, 1)[0] + dealt(nc.vector, "w2_s0", w2_sraw, U8, 0, 1)[0]]
        w2_w = w2_w + dealt(nc.gpsimd, "w2_w1", w2_raw[:], U32, 1, PACK)
        for t in range(1, PACK):
            sc = sc + dealt(nc.gpsimd, f"sc{t}", raw_s[:], U8, t, t + 1)
        w_op = [(w_w[t][0].bitcast(E5M2), sc[t][0]) for t in range(PACK)]
        w2_op = [(w2_w[t][0].bitcast(E5M2), sc[t][1]) for t in range(PACK)]

        def mm(dst, stat, mov, start, stop):
            nc.tensor.matmul_mx(out=dst, lhsT=stat[0], lhsT_scale=stat[1], rhs=mov[0], rhs_scale=mov[1], start=start, stop=stop)

        def sum_a(dst, t):
            mm(dst, w_op[t], xt_op, True, False)
            mm(dst, w2_op[t], xo_op, False, True)

        def sum_b(dst, t):
            mm(dst, w2_op[t], xt_op, True, False)
            mm(dst, w_op[t], xo_op, False, True)

        a_ps, b_ps = ps.tile([P, J], F32, name="a0", tag="a0"), ps.tile([P, J], F32, name="b0", tag="b0")
        mm(a_ps[:], w_op[0], xt_op, True, False)
        mm(b_ps[:], w_op[0], xo_op, True, False)
        mm(a_ps[:], w2_op[0], xo_op, False, True)
        mm(b_ps[:], w2_op[0], xt_op, False, True)
        first_a = tile("first_a", [P, J], F32, tag="staged_a")
        first_b = tile("first_b", [P, J], F32, tag="staged_b")
        nc.scalar.copy(first_a[:], a_ps[:])
        nc.vector.tensor_copy(first_b[:], b_ps[:])
        a_sb, b_sb = [first_a[:]], [first_b[:]]

        def put_a(t):
            nc.scalar.activation(out=pw[t][:].indirect(l3[:]), in_=a_sb[t], func=COPY)

        def put_b(t):
            nc.vector.tensor_copy(pv[t][:].indirect(l4[:]), b_sb[t])

        halves = 2
        half = O // halves
        last = PACK - 1

        put_a(0)
        put_b(0)

        def later_sums(kind, summed, copy, staged):
            later = tile(f"later_{kind}", [P, last * J], F32, tag=f"staged_{kind}")
            for first, stop in ((1, last), (last, PACK)):
                bank = ps.tile([P, (stop - first) * J], F32, name=f"{kind}{first}")
                for t in range(first, stop):
                    summed(bank[:, (t - first) * J : (t - first + 1) * J], t)
                    staged.append(later[:, (t - 1) * J : t * J])
                copy(later[:, (first - 1) * J : (stop - 1) * J], bank[:])

        later_sums("a", sum_a, nc.scalar.copy, a_sb)
        later_sums("b", sum_b, nc.vector.tensor_copy, b_sb)
        for t in range(1, PACK):
            put_a(t)
            put_b(t)

        p_ps = [[ps.tile([P, half], F32, name=f"p{h}{u}", tag=("a0", "b0")[h] if u == 0 else f"p{h}") for u in range(halves)] for h in range(N // P)]
        for u in range(halves):
            reads = slice(half * u, half * (u + 1))
            for h in range(N // P):
                cols = slice(P * h, P * (h + 1))
                mm(p_ps[h][u][:], (ws_w[:, cols].bitcast(E5M2), ws_s[:, cols]), (sx_w[:, reads].bitcast(E2M1), sx_s[:, reads]), True, False)

        pg = [tile(f"pg{t}", [P, C], F32) for t in range(PACK)]
        for t in range(PACK):
            (nc.vector if t == last else nc.gpsimd).tensor_tensor(pg[t][:], pw[t][:], pv[t][:], ADD)
        low = tile("low", [P, 2 * O], BF16, tag="staged_a")
        high = tile("high", [P, 2 * O], BF16, tag="staged_b")
        for t, dst in enumerate((low[:, 0:O], low[:, O:], high[:, 0:O])):
            nc.scalar.activation(out=dst, in_=pg[t][:].indirect(l5[:]), func=COPY)
        nc.vector.tensor_copy(high[:, O:], pg[last][:].indirect(l5[:]))

        woven = [tile(f"hid{u}", [P, half * PACK], BF16, tag=(f"pv{last}", f"pw{last}")[u]) for u in range(halves)]
        for i, pair in enumerate((low, high)):
            for u in range(halves):
                src = pair[:].rearrange("p (e o) -> p o e", e=2)[:, half * u : half * (u + 1), :]
                nc.vector.tensor_copy(woven[u][:].rearrange("p (o t) -> p o t", t=PACK)[:, :, 2 * i : 2 * i + 2], src)
        for u in range(halves):
            hid_w = tile(f"hid_w{u}", [P, half], U32)
            hid_s = tile(f"hid_s{u}", [P, half], U8)
            nc.vector.quantize_mx(out=hid_w[:].bitcast(E4M3), scales=hid_s[:], in_=woven[u][:])
            for h in range(N // P):
                cols = slice(P * h, P * (h + 1))
                mm(p_ps[h][u][:], (wb_w[:, cols].bitcast(E5M2), wb_s[:, cols]),
                   (hid_w[:].bitcast(E4M3), hid_s[:]), False, True)

        for h in range(N // P):
            p_sb = tile(f"p_sb{h}", [P, O], F32)
            g6 = tile(f"g6_{h}", [P, E], F32)
            g7 = tile(f"g7_{h}", [P, E], F32)
            res = tile(f"res{h}", [P, E], F32)
            if h == 0:
                for u in range(halves):
                    nc.scalar.copy(p_sb[:, half * u : half * (u + 1)], p_ps[h][u][:])
                nc.scalar.activation(out=g6[:], in_=p_sb[:].indirect(l6[:]), func=COPY)
                nc.scalar.activation(out=g7[:], in_=p_sb[:].indirect(l7[:]), func=COPY)
            else:
                for u in range(halves):
                    nc.vector.tensor_copy(p_sb[:, half * u : half * (u + 1)], p_ps[h][u][:])
                nc.vector.tensor_copy(g6[:], p_sb[:].indirect(l6[:]))
                nc.vector.tensor_copy(g7[:], p_sb[:].indirect(l7[:]))
            nc.vector.tensor_tensor(res[:], g6[:], g7[:], MAX)
            nc.sync.dma_start(out[P * h : P * (h + 1), :], res[:])
